import numpy as np
import ml_dtypes


def mxq(x, axis, fmt="e4m3"):
    dtype, down = {"e4m3": (ml_dtypes.float8_e4m3fn, 7), "e5m2": (ml_dtypes.float8_e5m2, 14)}[fmt]
    v = np.moveaxis(np.asarray(x, np.float32).astype(ml_dtypes.bfloat16).astype(np.float64), axis, -1)
    blocks = v.reshape(v.shape[:-1] + (-1, 32))
    amax = np.abs(blocks).max(-1, keepdims=True)
    byte = np.maximum(np.where(amax > 0, np.frexp(amax)[1] - 1 + 127, 0) - down, 1)
    scale = np.exp2(byte - 127.0)
    codes = (blocks / scale).astype(np.float32).astype(dtype).astype(np.float64)
    return np.moveaxis((codes * scale).reshape(v.shape), -1, axis)


WIDE = False


def mx_kscale(k):
    if not WIDE:
        return np.ones(k)
    levels = np.array([30, -30])
    if k % 512:
        return np.exp2(np.random.permutation(np.resize(levels, k // 32))).repeat(32)
    a = np.empty((k // 512, 16))
    for p in range(k // 512):
        a[p, :8] = np.random.permutation(np.resize(levels, 8))
        for g in range(8):
            far = levels[np.abs(levels - a[p, g]) >= 10]
            a[p, g + 8] = far[np.random.randint(len(far))]
    return np.exp2(a.ravel()).repeat(32)


def f64(x):
    return np.asarray(x).astype(np.float64)


def striped(idx):
    return np.tile(idx.reshape(-1, 16).T, (8, 1)).astype(np.uint16)


def unstriped(offs):
    return offs[:16].T.reshape(-1).astype(np.int64)


K, T, E, C, N = 384, 1536, 2, 512, 1024


def by_expert(wq, xq):
    return np.concatenate([wq[e].T @ xq[:, e * C:(e + 1) * C] for e in range(E)], axis=1)


def setup_inputs():
    n = np.random.standard_normal
    s = mx_kscale(N)[:, None]
    return {
        "dyT": (n((N, T)) * s).astype(np.float32),
        "w": (n((E + 1, N, K)) / np.sqrt(N) / s[None]).astype(np.float32),
        "gate": np.tile(np.random.uniform(0.2, 1.0, E * C), (N, 1)).astype(np.float32),
        "offs": striped(np.random.permutation(T)[:E * C]),
    }


def reference(dyT, w, gate, offs):
    idx = unstriped(offs)
    gq = mxq(f64(gate) * f64(dyT)[:, idx], 0, "e5m2")
    wq = mxq(f64(w), 1, "e4m3")
    ds = wq[E].T @ mxq(f64(dyT), 0, "e5m2")
    dx = by_expert(wq, gq)
    ds[:, idx] += dx
    return ds

@@ -1,0 +1,220 @@
+from contextlib import ExitStack
+
+import concourse.mybir as mybir
+
+K, T, E, C, N = 384, 1536, 2, 512, 1024
+FLOPS = 2 * N * K * (E * C + T)
+BYTES = 4 * (N * T + (E + 1) * N * K + 128 * E * C + K * T) + 2 * 128 * (E * C // 16)
+
+F32 = mybir.dt.float32
+BF16 = mybir.dt.bfloat16
+U32 = mybir.dt.uint32
+U16 = mybir.dt.uint16
+U8 = mybir.dt.uint8
+E4M3 = mybir.dt.float8_e4m3fn_x4
+E5M2 = mybir.dt.float8_e5m2_x4
+MULT = mybir.AluOpType.mult
+ADD = mybir.AluOpType.add
+
+P = 128
+PACK = 4
+PASSES = N // (P * PACK)
+K_TILES = K // P
+CHUNK = 512
+CHUNKS = T // CHUNK
+SHARED = E
+RUN = 4
+
+
+def tile_moe_bds_lin_none_kernel(tc, dyT, w, gate, offs, out):
+    nc = tc.nc
+    with ExitStack() as ctx:
+        keep = ctx.enter_context(tc.tile_pool(name="keep", bufs=1))
+        w_ring = ctx.enter_context(tc.tile_pool(name="w_ring", bufs=4))
+        raw_ring = ctx.enter_context(tc.tile_pool(name="raw_ring", bufs=6))
+        bf_ring = ctx.enter_context(tc.tile_pool(name="bf_ring", bufs=7))
+        wbf_ring = ctx.enter_context(tc.tile_pool(name="wbf_ring", bufs=2))
+        psum = ctx.enter_context(tc.psum_pool(name="psum", bufs=8))
+
+        dy_rows = dyT.rearrange("(a p t) c -> a p t c", p=P, t=PACK)
+        w_rows = w.rearrange("e (a p t) k -> e a p t k", p=P, t=PACK)
+
+        offsets = keep.tile([P, E * C // 16], U16, name="offsets")
+        gates = [keep.tile([P, C], F32, name=f"gate{e}") for e in range(E)]
+        planes = {(a, t): keep.tile([P, T], F32, name=f"plane{a}{t}") for a in range(PASSES) for t in range(PACK)}
+        windows = [keep.tile([P, T], F32, name=f"window{kt}") for kt in range(K_TILES)]
+        w_codes = [keep.tile([P, PASSES * K], U32, name=f"w_codes{m}", align_bytes=64) for m in range(E + 1)]
+        w_scales = [keep.tile([P, PASSES * K], U8, name=f"w_scales{m}", align_bytes=64) for m in range(E + 1)]
+        g_codes = {(e, a): keep.tile([P, C], U32, name=f"g_codes{e}{a}", align_bytes=64) for e in range(E) for a in range(PASSES)}
+        g_scales = {(e, a): keep.tile([P, C], U8, name=f"g_scales{e}{a}", align_bytes=64) for e in range(E) for a in range(PASSES)}
+        dy_codes = [keep.tile([P, PASSES * CHUNK], U32, name=f"dy_codes{c}", align_bytes=64) for c in range(CHUNKS)]
+        dy_scales = [keep.tile([P, PASSES * CHUNK], U8, name=f"dy_scales{c}", align_bytes=64) for c in range(CHUNKS)]
+        dx = {(e, kt): keep.tile([P, C], F32, name=f"dx{e}{kt}") for e in range(E) for kt in range(K_TILES)}
+
+        w_raw, dy_raw, g_raw, w_bf, g_bf, dy_bf, dx_banks = {}, {}, {}, {}, {}, {}, {}
+
+        def slots(e):
+            return offsets[:, e * C // 16 : (e + 1) * C // 16]
+
+        def load_gate(e):
+            nc.sync.dma_start(gates[e][:], gate[0:P, e * C : (e + 1) * C])
+
+        def load_plane(a, t):
+            nc.sync.dma_start(planes[a, t][:], dy_rows[a, :, t, :])
+
+        def load_w(m, a):
+            w_raw[m, a] = w_ring.tile([P, PACK, K], F32, name="w_raw")
+            nc.sync.dma_start(w_raw[m, a][:], w_rows[m, a])
+
+        def load_dy(c, a):
+            dy_raw[c, a] = raw_ring.tile([P, PACK, CHUNK], F32, name="raw")
+            nc.sync.dma_start(dy_raw[c, a][:], dy_rows[a, :, :, c * CHUNK : (c + 1) * CHUNK])
+
+        def interleave(dst, src):
+            nc.scalar.copy(
+                dst.rearrange("p (c i t) -> p c t i", i=RUN, t=PACK),
+                src.rearrange("p t (c i) -> p c t i", i=RUN),
+            )
+
+        def gather(e, a, t):
+            if t == 0:
+                g_raw[e, a] = raw_ring.tile([P, PACK, C], F32, name="raw")
+            nc.vector.tensor_tensor(g_raw[e, a][:, t, :], planes[a, t][:].indirect(slots(e)), gates[e][:], MULT)
+
+        def interleave_g(e, a):
+            g_bf[e, a] = bf_ring.tile([P, C * PACK], BF16, name="bf", align_bytes=64)
+            interleave(g_bf[e, a][:], g_raw[e, a][:])
+
+        def quantize_g(e, a):
+            nc.vector.quantize_mx(g_codes[e, a][:].bitcast(E5M2), g_scales[e, a][:], g_bf[e, a][:])
+
+        def interleave_w(m, a):
+            if a == 0:
+                w_bf[m] = wbf_ring.tile([P, PASSES * K * PACK], BF16, name="w_bf", align_bytes=64)
+            interleave(w_bf[m][:, a * K * PACK : (a + 1) * K * PACK], w_raw[m, a][:])
+
+        def quantize_w(m):
+            for lo, hi in ((0, 512), (512, PASSES * K)):
+                nc.vector.quantize_mx(w_codes[m][:, lo:hi].bitcast(E4M3), w_scales[m][:, lo:hi], w_bf[m][:, PACK * lo : PACK * hi])
+
+        def interleave_dy(c, a):
+            dy_bf[c, a] = bf_ring.tile([P, CHUNK * PACK], BF16, name="bf", align_bytes=64)
+            interleave(dy_bf[c, a][:], dy_raw[c, a][:])
+
+        def quantize_dy(c):
+            for a in range(PASSES):
+                cols = slice(a * CHUNK, (a + 1) * CHUNK)
+                nc.vector.quantize_mx(dy_codes[c][:, cols].bitcast(E5M2), dy_scales[c][:, cols], dy_bf[c, a][:])
+
+        def product(m, kt, moving):
+            bank = psum.tile([P, CHUNK], F32, name="bank")
+            for a in range(PASSES):
+                cols = slice(a * K + kt * P, a * K + (kt + 1) * P)
+                codes, scales = moving(a)
+                nc.tensor.matmul_mx(
+                    bank[:],
+                    lhsT=w_codes[m][:, cols].bitcast(E4M3),
+                    lhsT_scale=w_scales[m][:, cols],
+                    rhs=codes.bitcast(E5M2),
+                    rhs_scale=scales,
+                    start=(a == 0),
+                    stop=(a == PASSES - 1),
+                )
+            return bank
+
+        def expert(e):
+            for kt in range(K_TILES):
+                bank = product(e, kt, lambda a: (g_codes[e, a][:], g_scales[e, a][:]))
+                nc.scalar.copy(dx[e, kt][:], bank[:])
+
+        def scatter(e, kt):
+            nc.vector.tensor_copy(windows[kt][:].indirect(slots(e)), dx[e, kt][:])
+
+        def finish(kt, c):
+            def moving(a):
+                cols = slice(a * CHUNK, (a + 1) * CHUNK)
+                return dy_codes[c][:, cols], dy_scales[c][:, cols]
+
+            bank = product(SHARED, kt, moving)
+            cols = slice(c * CHUNK, (c + 1) * CHUNK)
+            nc.vector.tensor_tensor(windows[kt][:, cols], bank[:], windows[kt][:, cols], ADD)
+            nc.sync.dma_start(out[kt * P : (kt + 1) * P, cols], windows[kt][:, cols])
+
+        nc.sync.dma_start(offsets[:], offs)
+        load_gate(0)
+        load_plane(0, 0)
+        load_gate(1)
+        load_plane(0, 1)
+        load_plane(0, 2)
+        load_w(0, 0)
+        load_plane(0, 3)
+        load_plane(1, 0)
+        load_plane(1, 1)
+        load_w(0, 1)
+        load_plane(1, 2)
+        load_plane(1, 3)
+        load_w(1, 0)
+        load_w(1, 1)
+
+        for kt in range(K_TILES):
+            nc.vector.memset(windows[kt][:], 0.0)
+
+        for t in range(PACK):
+            for e in range(E):
+                gather(e, 0, t)
+        interleave_w(0, 0)
+        interleave_g(0, 0)
+        interleave_g(1, 0)
+        interleave_w(0, 1)
+        gather(0, 1, 0)
+        quantize_g(0, 0)
+        gather(0, 1, 1)
+        gather(1, 1, 0)
+        quantize_g(1, 0)
+        gather(0, 1, 2)
+        gather(0, 1, 3)
+        interleave_g(0, 1)
+        gather(1, 1, 1)
+        quantize_w(0)
+        gather(1, 1, 2)
+        quantize_g(0, 1)
+        gather(1, 1, 3)
+        load_w(SHARED, 0)
+        load_w(SHARED, 1)
+        load_dy(0, 0)
+        load_dy(0, 1)
+        interleave_w(1, 0)
+        expert(0)
+        interleave_g(1, 1)
+        interleave_w(1, 1)
+        scatter(0, 0)
+        quantize_g(1, 1)
+        scatter(0, 1)
+        quantize_w(1)
+        interleave_w(SHARED, 0)
+        expert(1)
+        interleave_w(SHARED, 1)
+        load_dy(1, 0)
+        load_dy(1, 1)
+        load_dy(2, 0)
+        load_dy(2, 1)
+        interleave_dy(0, 0)
+        interleave_dy(0, 1)
+        scatter(0, 2)
+        quantize_w(SHARED)
+        scatter(1, 0)
+        interleave_dy(1, 0)
+        interleave_dy(1, 1)
+        quantize_dy(0)
+        scatter(1, 1)
+        interleave_dy(2, 0)
+        interleave_dy(2, 1)
+        finish(0, 0)
+        finish(1, 0)
+        quantize_dy(1)
+        scatter(1, 2)
+        finish(2, 0)
+        quantize_dy(2)
+        for c in range(1, CHUNKS):
+            for kt in range(K_TILES):
+                finish(kt, c)

@@ -32,7 +32,7 @@ def tile_moe_bds_lin_none_kernel(tc, dyT, w, gate, offs, out):
         keep = ctx.enter_context(tc.tile_pool(name="keep", bufs=1))
         w_ring = ctx.enter_context(tc.tile_pool(name="w_ring", bufs=4))
         raw_ring = ctx.enter_context(tc.tile_pool(name="raw_ring", bufs=6))
-        bf_ring = ctx.enter_context(tc.tile_pool(name="bf_ring", bufs=7))
+        bf_ring = ctx.enter_context(tc.tile_pool(name="bf_ring", bufs=5))
         wbf_ring = ctx.enter_context(tc.tile_pool(name="wbf_ring", bufs=2))
         psum = ctx.enter_context(tc.psum_pool(name="psum", bufs=8))
 
@@ -40,7 +40,9 @@ def tile_moe_bds_lin_none_kernel(tc, dyT, w, gate, offs, out):
         w_rows = w.rearrange("e (a p t) k -> e a p t k", p=P, t=PACK)
 
         offsets = keep.tile([P, E * C // 16], U16, name="offsets")
-        gates = [keep.tile([P, C], F32, name=f"gate{e}") for e in range(E)]
+        shared_bytes = keep.tile([P, PACK * C], F32, name="shared_bytes", align_bytes=64)
+        gate1 = keep.tile([P, C], F32, name="gate1")
+        gates = [shared_bytes[:, C // 2 : C // 2 + C], gate1[:]]
         planes = {(a, t): keep.tile([P, T], F32, name=f"plane{a}{t}") for a in range(PASSES) for t in range(PACK)}
         windows = [keep.tile([P, T], F32, name=f"window{kt}") for kt in range(K_TILES)]
         w_codes = [keep.tile([P, PASSES * K], U32, name=f"w_codes{m}", align_bytes=64) for m in range(E + 1)]
@@ -57,7 +59,7 @@ def tile_moe_bds_lin_none_kernel(tc, dyT, w, gate, offs, out):
             return offsets[:, e * C // 16 : (e + 1) * C // 16]
 
         def load_gate(e):
-            nc.sync.dma_start(gates[e][:], gate[0:P, e * C : (e + 1) * C])
+            nc.sync.dma_start(gates[e], gate[0:P, e * C : (e + 1) * C])
 
         def load_plane(a, t):
             nc.sync.dma_start(planes[a, t][:], dy_rows[a, :, t, :])
@@ -77,16 +79,21 @@ def tile_moe_bds_lin_none_kernel(tc, dyT, w, gate, offs, out):
             )
 
         def gather(e, a, t):
-            if t == 0:
-                g_raw[e, a] = raw_ring.tile([P, PACK, C], F32, name="raw")
-            nc.vector.tensor_tensor(g_raw[e, a][:, t, :], planes[a, t][:].indirect(slots(e)), gates[e][:], MULT)
+            if t == 0 and (e, a) == (1, 1):
+                g_raw[e, a] = shared_bytes[:].rearrange("p (t c) -> p t c", t=PACK)
+            elif t == 0:
+                g_raw[e, a] = raw_ring.tile([P, PACK, C], F32, name="raw")[:]
+            nc.vector.tensor_tensor(g_raw[e, a][:, t, :], planes[a, t][:].indirect(slots(e)), gates[e], MULT)
 
         def interleave_g(e, a):
-            g_bf[e, a] = bf_ring.tile([P, C * PACK], BF16, name="bf", align_bytes=64)
-            interleave(g_bf[e, a][:], g_raw[e, a][:])
+            if (e, a) == (0, 1):
+                g_bf[e, a] = shared_bytes[:, 2 * C :].bitcast(BF16)
+            else:
+                g_bf[e, a] = bf_ring.tile([P, C * PACK], BF16, name="bf", align_bytes=64)[:]
+            interleave(g_bf[e, a], g_raw[e, a])
 
         def quantize_g(e, a):
-            nc.vector.quantize_mx(g_codes[e, a][:].bitcast(E5M2), g_scales[e, a][:], g_bf[e, a][:])
+            nc.vector.quantize_mx(g_codes[e, a][:].bitcast(E5M2), g_scales[e, a][:], g_bf[e, a])
 
         def interleave_w(m, a):
             if a == 0:
@@ -101,10 +108,9 @@ def tile_moe_bds_lin_none_kernel(tc, dyT, w, gate, offs, out):
             dy_bf[c, a] = bf_ring.tile([P, CHUNK * PACK], BF16, name="bf", align_bytes=64)
             interleave(dy_bf[c, a][:], dy_raw[c, a][:])
 
-        def quantize_dy(c):
-            for a in range(PASSES):
-                cols = slice(a * CHUNK, (a + 1) * CHUNK)
-                nc.vector.quantize_mx(dy_codes[c][:, cols].bitcast(E5M2), dy_scales[c][:, cols], dy_bf[c, a][:])
+        def quantize_dy(c, a):
+            cols = slice(a * CHUNK, (a + 1) * CHUNK)
+            nc.vector.quantize_mx(dy_codes[c][:, cols].bitcast(E5M2), dy_scales[c][:, cols], dy_bf[c, a][:])
 
         def product(m, kt, moving):
             bank = psum.tile([P, CHUNK], F32, name="bank")
@@ -122,10 +128,11 @@ def tile_moe_bds_lin_none_kernel(tc, dyT, w, gate, offs, out):
                 )
             return bank
 
-        def expert(e):
-            for kt in range(K_TILES):
-                bank = product(e, kt, lambda a: (g_codes[e, a][:], g_scales[e, a][:]))
-                nc.scalar.copy(dx[e, kt][:], bank[:])
+        def expert(e, kt):
+            dx_banks[e, kt] = product(e, kt, lambda a: (g_codes[e, a][:], g_scales[e, a][:]))
+
+        def evacuate(e, kt):
+            nc.scalar.copy(dx[e, kt][:], dx_banks[e, kt][:])
 
         def scatter(e, kt):
             nc.vector.tensor_copy(windows[kt][:].indirect(slots(e)), dx[e, kt][:])
@@ -155,13 +162,19 @@ def tile_moe_bds_lin_none_kernel(tc, dyT, w, gate, offs, out):
         load_plane(1, 3)
         load_w(1, 0)
         load_w(1, 1)
-
-        for kt in range(K_TILES):
-            nc.vector.memset(windows[kt][:], 0.0)
-
-        for t in range(PACK):
-            for e in range(E):
-                gather(e, 0, t)
+        load_w(2, 0)
+        load_w(2, 1)
+        nc.gpsimd.memset(windows[0][:], 0.0)
+        nc.gpsimd.memset(windows[1][:], 0.0)
+        nc.gpsimd.memset(windows[2][:], 0.0)
+        gather(0, 0, 0)
+        gather(1, 0, 0)
+        gather(0, 0, 1)
+        gather(1, 0, 1)
+        gather(0, 0, 2)
+        gather(1, 0, 2)
+        gather(0, 0, 3)
+        gather(1, 0, 3)
         interleave_w(0, 0)
         interleave_g(0, 0)
         interleave_g(1, 0)
@@ -169,52 +182,66 @@ def tile_moe_bds_lin_none_kernel(tc, dyT, w, gate, offs, out):
         gather(0, 1, 0)
         quantize_g(0, 0)
         gather(0, 1, 1)
-        gather(1, 1, 0)
         quantize_g(1, 0)
+        quantize_w(0)
         gather(0, 1, 2)
         gather(0, 1, 3)
         interleave_g(0, 1)
+        gather(1, 1, 0)
         gather(1, 1, 1)
-        quantize_w(0)
-        gather(1, 1, 2)
         quantize_g(0, 1)
+        gather(1, 1, 2)
         gather(1, 1, 3)
-        load_w(SHARED, 0)
-        load_w(SHARED, 1)
         load_dy(0, 0)
         load_dy(0, 1)
-        interleave_w(1, 0)
-        expert(0)
-        interleave_g(1, 1)
-        interleave_w(1, 1)
-        scatter(0, 0)
-        quantize_g(1, 1)
-        scatter(0, 1)
-        quantize_w(1)
-        interleave_w(SHARED, 0)
-        expert(1)
-        interleave_w(SHARED, 1)
         load_dy(1, 0)
         load_dy(1, 1)
         load_dy(2, 0)
         load_dy(2, 1)
-        interleave_dy(0, 0)
-        interleave_dy(0, 1)
+        interleave_w(1, 0)
+        expert(0, 0)
+        expert(0, 1)
+        expert(0, 2)
+        evacuate(0, 0)
+        scatter(0, 0)
+        interleave_g(1, 1)
+        quantize_g(1, 1)
+        interleave_w(1, 1)
+        quantize_w(1)
+        evacuate(0, 1)
+        scatter(0, 1)
+        expert(1, 0)
+        expert(1, 1)
+        expert(1, 2)
+        interleave_w(2, 0)
+        interleave_w(2, 1)
+        quantize_w(2)
+        evacuate(0, 2)
         scatter(0, 2)
-        quantize_w(SHARED)
+        interleave_dy(0, 0)
+        quantize_dy(0, 0)
+        interleave_dy(0, 1)
+        quantize_dy(0, 1)
+        evacuate(1, 0)
         scatter(1, 0)
-        interleave_dy(1, 0)
-        interleave_dy(1, 1)
-        quantize_dy(0)
-        scatter(1, 1)
-        interleave_dy(2, 0)
-        interleave_dy(2, 1)
         finish(0, 0)
+        interleave_dy(1, 0)
+        quantize_dy(1, 0)
+        interleave_dy(1, 1)
+        quantize_dy(1, 1)
+        evacuate(1, 1)
+        scatter(1, 1)
         finish(1, 0)
-        quantize_dy(1)
+        finish(0, 1)
+        finish(1, 1)
+        interleave_dy(2, 0)
+        quantize_dy(2, 0)
+        interleave_dy(2, 1)
+        quantize_dy(2, 1)
+        evacuate(1, 2)
         scatter(1, 2)
         finish(2, 0)
-        quantize_dy(2)
-        for c in range(1, CHUNKS):
-            for kt in range(K_TILES):
-                finish(kt, c)
+        finish(0, 2)
+        finish(1, 2)
+        finish(2, 1)
+        finish(2, 2)

@@ -1,6 +1,7 @@
 from contextlib import ExitStack
 
 import concourse.mybir as mybir
+from concourse.masks import make_identity
 
 K, T, E, C, N = 384, 1536, 2, 512, 1024
 FLOPS = 2 * N * K * (E * C + T)
@@ -31,9 +32,8 @@ def tile_moe_bds_lin_none_kernel(tc, dyT, w, gate, offs, out):
     with ExitStack() as ctx:
         keep = ctx.enter_context(tc.tile_pool(name="keep", bufs=1))
         w_ring = ctx.enter_context(tc.tile_pool(name="w_ring", bufs=4))
-        raw_ring = ctx.enter_context(tc.tile_pool(name="raw_ring", bufs=6))
-        bf_ring = ctx.enter_context(tc.tile_pool(name="bf_ring", bufs=5))
-        wbf_ring = ctx.enter_context(tc.tile_pool(name="wbf_ring", bufs=2))
+        raw_ring = ctx.enter_context(tc.tile_pool(name="raw_ring", bufs=3))
+        dx_ring = ctx.enter_context(tc.tile_pool(name="dx_ring", bufs=3))
         psum = ctx.enter_context(tc.psum_pool(name="psum", bufs=8))
 
         dy_rows = dyT.rearrange("(a p t) c -> a p t c", p=P, t=PACK)
@@ -41,8 +41,14 @@ def tile_moe_bds_lin_none_kernel(tc, dyT, w, gate, offs, out):
 
         offsets = keep.tile([P, E * C // 16], U16, name="offsets")
         shared_bytes = keep.tile([P, PACK * C], F32, name="shared_bytes", align_bytes=64)
-        gate1 = keep.tile([P, C], F32, name="gate1")
-        gates = [shared_bytes[:, C // 2 : C // 2 + C], gate1[:]]
+        shared_bytes2 = keep.tile([P, 3072], F32, name="shared_bytes2", align_bytes=64)
+        pair_a = keep.tile([P, 4096], F32, name="pair_a")
+        pair_b = keep.tile([P, 4352], F32, name="pair_b")
+        units = keep.tile([P, 4096], F32, name="units", align_bytes=64)
+        gates = [shared_bytes[:, C // 2 : C // 2 + C], shared_bytes2[:, 1536:2048]]
+        gate_cols = keep.tile([P, E, PACK], F32, name="gate_cols")
+        w_stage = [keep.tile([P, PASSES * K * PACK // 2], F32, name="w_stage", align_bytes=64)[:], shared_bytes2[:, 0:1536]]
+        identity = keep.tile([P, P], F32, name="identity")[:]
         planes = {(a, t): keep.tile([P, T], F32, name=f"plane{a}{t}") for a in range(PASSES) for t in range(PACK)}
         windows = [keep.tile([P, T], F32, name=f"window{kt}") for kt in range(K_TILES)]
         w_codes = [keep.tile([P, PASSES * K], U32, name=f"w_codes{m}", align_bytes=64) for m in range(E + 1)]
@@ -51,32 +57,47 @@ def tile_moe_bds_lin_none_kernel(tc, dyT, w, gate, offs, out):
         g_scales = {(e, a): keep.tile([P, C], U8, name=f"g_scales{e}{a}", align_bytes=64) for e in range(E) for a in range(PASSES)}
         dy_codes = [keep.tile([P, PASSES * CHUNK], U32, name=f"dy_codes{c}", align_bytes=64) for c in range(CHUNKS)]
         dy_scales = [keep.tile([P, PASSES * CHUNK], U8, name=f"dy_scales{c}", align_bytes=64) for c in range(CHUNKS)]
-        dx = {(e, kt): keep.tile([P, C], F32, name=f"dx{e}{kt}") for e in range(E) for kt in range(K_TILES)}
+        dx, ds, ds_banks = {}, {}, {}
 
         w_raw, dy_raw, g_raw, w_bf, g_bf, dy_bf, dx_banks = {}, {}, {}, {}, {}, {}, {}
 
         def slots(e):
             return offsets[:, e * C // 16 : (e + 1) * C // 16]
 
-        def load_gate(e):
-            nc.sync.dma_start(gates[e], gate[0:P, e * C : (e + 1) * C])
+        def load_gate():
+            nc.sync.dma_start(gate_cols[:], gate[0, :].rearrange("(e p i) -> p e i", e=E, i=PACK))
+            make_identity(nc, identity)
+
+        def spread_gate(e):
+            bank = psum.tile([P, CHUNK], F32, name="bank")
+            for i in range(PACK):
+                nc.tensor.transpose(bank[:, i * P : (i + 1) * P], gate_cols[:, e, i : i + 1].to_broadcast([P, P]), identity)
+            nc.vector.tensor_copy(gates[e].rearrange("q (p i) -> q p i", i=PACK), bank[:].rearrange("q (i p) -> q p i", i=PACK))
 
         def load_plane(a, t):
             nc.sync.dma_start(planes[a, t][:], dy_rows[a, :, t, :])
 
         def load_w(m, a):
-            w_raw[m, a] = w_ring.tile([P, PACK, K], F32, name="w_raw")
-            nc.sync.dma_start(w_raw[m, a][:], w_rows[m, a])
+            w_raw[m, a] = w_ring.tile([P, PACK, K], F32, name="w_raw")[:]
+            nc.sync.dma_start(w_raw[m, a], w_rows[m, a])
 
         def load_dy(c, a):
-            dy_raw[c, a] = raw_ring.tile([P, PACK, CHUNK], F32, name="raw")
-            nc.sync.dma_start(dy_raw[c, a][:], dy_rows[a, :, :, c * CHUNK : (c + 1) * CHUNK])
+            if c == 0:
+                dy_raw[c, a] = pair_a[:].rearrange("p (t h c) -> p t h c", t=PACK, h=2)[:, :, a, :]
+            elif (c, a) in ((1, 1), (2, 0)):
+                dy_raw[c, a] = pair_b[:, 0:4096].rearrange("p (t h c) -> p t h c", t=PACK, h=2)[:, :, a, :]
+            else:
+                dy_raw[c, a] = raw_ring.tile([P, PACK, CHUNK], F32, name="raw")[:]
+            nc.sync.dma_start(dy_raw[c, a], dy_rows[a, :, :, c * CHUNK : (c + 1) * CHUNK])
 
         def interleave(dst, src):
             nc.scalar.copy(
                 dst.rearrange("p (c i t) -> p c t i", i=RUN, t=PACK),
                 src.rearrange("p t (c i) -> p c t i", i=RUN),
             )
+
+        def interleave_gpsimd(dst, src):
+            nc.gpsimd.tensor_scalar(dst.rearrange("p (c t) -> p c t", t=PACK), src.rearrange("p t c -> p c t"), 1.0, 0.0, MULT, ADD)
 
         def gather(e, a, t):
             if t == 0 and (e, a) == (1, 1):
@@ -88,29 +109,34 @@ def tile_moe_bds_lin_none_kernel(tc, dyT, w, gate, offs, out):
         def interleave_g(e, a):
             if (e, a) == (0, 1):
                 g_bf[e, a] = shared_bytes[:, 2 * C :].bitcast(BF16)
+            elif (e, a) == (1, 1):
+                g_bf[e, a] = shared_bytes2[:, 2048:3072].bitcast(BF16)
             else:
-                g_bf[e, a] = bf_ring.tile([P, C * PACK], BF16, name="bf", align_bytes=64)[:]
+                g_bf[e, a] = units[:, e * 1024 : (e + 1) * 1024].bitcast(BF16)
             interleave(g_bf[e, a], g_raw[e, a])
 
         def quantize_g(e, a):
             nc.vector.quantize_mx(g_codes[e, a][:].bitcast(E5M2), g_scales[e, a][:], g_bf[e, a])
 
         def interleave_w(m, a):
-            if a == 0:
-                w_bf[m] = wbf_ring.tile([P, PASSES * K * PACK], BF16, name="w_bf", align_bytes=64)
-            interleave(w_bf[m][:, a * K * PACK : (a + 1) * K * PACK], w_raw[m, a][:])
+            w_bf[m] = w_stage[m].bitcast(BF16)
+            interleave(w_bf[m][:, a * K * PACK : (a + 1) * K * PACK], w_raw[m, a])
+
+        def interleave_w_gpsimd(m, a):
+            w_bf[m] = shared_bytes2[:, 1280:2816].bitcast(BF16)
+            interleave_gpsimd(w_bf[m][:, a * K * PACK : (a + 1) * K * PACK], w_raw[m, a])
 
         def quantize_w(m):
             for lo, hi in ((0, 512), (512, PASSES * K)):
                 nc.vector.quantize_mx(w_codes[m][:, lo:hi].bitcast(E4M3), w_scales[m][:, lo:hi], w_bf[m][:, PACK * lo : PACK * hi])
 
         def interleave_dy(c, a):
-            dy_bf[c, a] = bf_ring.tile([P, CHUNK * PACK], BF16, name="bf", align_bytes=64)
-            interleave(dy_bf[c, a][:], dy_raw[c, a][:])
+            dy_bf[c] = (units[:, 1024:3072], units[:, 0:2048], units[:, 2048:4096])[c].bitcast(BF16)
+            step = interleave_gpsimd if (c, a) in ((0, 1), (1, 1)) else interleave
+            step(dy_bf[c][:, a * CHUNK * PACK : (a + 1) * CHUNK * PACK], dy_raw[c, a])
 
-        def quantize_dy(c, a):
-            cols = slice(a * CHUNK, (a + 1) * CHUNK)
-            nc.vector.quantize_mx(dy_codes[c][:, cols].bitcast(E5M2), dy_scales[c][:, cols], dy_bf[c, a][:])
+        def quantize_dy(c):
+            nc.vector.quantize_mx(dy_codes[c][:].bitcast(E5M2), dy_scales[c][:], dy_bf[c])
 
         def product(m, kt, moving):
             bank = psum.tile([P, CHUNK], F32, name="bank")
@@ -132,25 +158,53 @@ def tile_moe_bds_lin_none_kernel(tc, dyT, w, gate, offs, out):
             dx_banks[e, kt] = product(e, kt, lambda a: (g_codes[e, a][:], g_scales[e, a][:]))
 
         def evacuate(e, kt):
-            nc.scalar.copy(dx[e, kt][:], dx_banks[e, kt][:])
+            if (e, kt) == (1, 1):
+                dx[e, kt] = pair_a[:, 256:768]
+            elif kt == 2:
+                dx[e, kt] = pair_b[:, 256 + e * C : 256 + (e + 1) * C]
+            else:
+                dx[e, kt] = dx_ring.tile([P, C], F32, name="dx")[:]
+            nc.scalar.copy(dx[e, kt], dx_banks[e, kt][:])
 
         def scatter(e, kt):
-            nc.vector.tensor_copy(windows[kt][:].indirect(slots(e)), dx[e, kt][:])
+            nc.vector.tensor_copy(windows[kt][:].indirect(slots(e)), dx[e, kt])
 
-        def finish(kt, c):
+        def shared(kt, c):
             def moving(a):
                 cols = slice(a * CHUNK, (a + 1) * CHUNK)
                 return dy_codes[c][:, cols], dy_scales[c][:, cols]
 
-            bank = product(SHARED, kt, moving)
+            ds_banks[kt, c] = product(SHARED, kt, moving)
+
+        def evacuate_ds(kt, c):
+            place = 2 + 2 * c + kt
+            ds[kt, c] = pair_b[:, 256 + place * CHUNK : 256 + (place + 1) * CHUNK]
+            nc.scalar.copy(ds[kt, c], ds_banks[kt, c][:])
+
+        def add_gpsimd(kt, c):
+            cols = slice(c * CHUNK, (c + 1) * CHUNK)
+            if c == 2:
+                total = windows[kt][:, cols].rearrange("p (h c) -> p h c", h=2)
+            else:
+                place = 2 * c + kt
+                total = units[:, 1024:3072].rearrange("p (h c) -> p h c", h=2)[:, :, place * 256 : (place + 1) * 256]
+            nc.gpsimd.tensor_tensor(
+                total, ds[kt, c].rearrange("p (h c) -> p h c", h=2), windows[kt][:, cols].rearrange("p (h c) -> p h c", h=2), ADD
+            )
+            nc.scalar.dma_start(out[kt * P : (kt + 1) * P, cols].rearrange("p (h c) -> p h c", h=2), total)
+
+        def finish(kt, c):
+            shared(kt, c)
+            bank = ds_banks[kt, c]
             cols = slice(c * CHUNK, (c + 1) * CHUNK)
             nc.vector.tensor_tensor(windows[kt][:, cols], bank[:], windows[kt][:, cols], ADD)
             nc.sync.dma_start(out[kt * P : (kt + 1) * P, cols], windows[kt][:, cols])
 
+        load_gate()
         nc.sync.dma_start(offsets[:], offs)
-        load_gate(0)
         load_plane(0, 0)
-        load_gate(1)
+        spread_gate(0)
+        spread_gate(1)
         load_plane(0, 1)
         load_plane(0, 2)
         load_w(0, 0)
@@ -192,56 +246,65 @@ def tile_moe_bds_lin_none_kernel(tc, dyT, w, gate, offs, out):
         quantize_g(0, 1)
         gather(1, 1, 2)
         gather(1, 1, 3)
+        load_dy(2, 1)
         load_dy(0, 0)
         load_dy(0, 1)
         load_dy(1, 0)
         load_dy(1, 1)
         load_dy(2, 0)
-        load_dy(2, 1)
         interleave_w(1, 0)
+        interleave_w(1, 1)
+        quantize_w(1)
         expert(0, 0)
         expert(0, 1)
         expert(0, 2)
         evacuate(0, 0)
         scatter(0, 0)
+        interleave_w_gpsimd(2, 0)
         interleave_g(1, 1)
         quantize_g(1, 1)
-        interleave_w(1, 1)
-        quantize_w(1)
+        interleave_w_gpsimd(2, 1)
         evacuate(0, 1)
         scatter(0, 1)
         expert(1, 0)
         expert(1, 1)
         expert(1, 2)
-        interleave_w(2, 0)
-        interleave_w(2, 1)
-        quantize_w(2)
-        evacuate(0, 2)
-        scatter(0, 2)
-        interleave_dy(0, 0)
-        quantize_dy(0, 0)
         interleave_dy(0, 1)
-        quantize_dy(0, 1)
+        interleave_dy(2, 1)
         evacuate(1, 0)
         scatter(1, 0)
-        finish(0, 0)
+        quantize_w(2)
+        interleave_dy(0, 0)
         interleave_dy(1, 0)
-        quantize_dy(1, 0)
-        interleave_dy(1, 1)
-        quantize_dy(1, 1)
+        quantize_dy(0)
         evacuate(1, 1)
         scatter(1, 1)
-        finish(1, 0)
-        finish(0, 1)
-        finish(1, 1)
+        interleave_dy(1, 1)
         interleave_dy(2, 0)
-        quantize_dy(2, 0)
-        interleave_dy(2, 1)
-        quantize_dy(2, 1)
+        quantize_dy(2)
+        quantize_dy(1)
+        evacuate(0, 2)
+        scatter(0, 2)
         evacuate(1, 2)
         scatter(1, 2)
+        shared(0, 0)
+        evacuate_ds(0, 0)
+        add_gpsimd(0, 0)
+        shared(1, 0)
+        evacuate_ds(1, 0)
+        add_gpsimd(1, 0)
+        shared(0, 1)
+        evacuate_ds(0, 1)
+        add_gpsimd(0, 1)
+        shared(1, 1)
+        evacuate_ds(1, 1)
+        add_gpsimd(1, 1)
+        shared(0, 2)
+        evacuate_ds(0, 2)
+        add_gpsimd(0, 2)
+        shared(1, 2)
+        evacuate_ds(1, 2)
+        add_gpsimd(1, 2)
         finish(2, 0)
-        finish(0, 2)
-        finish(1, 2)
         finish(2, 1)
         finish(2, 2)

from contextlib import ExitStack

import concourse.mybir as mybir
from concourse.masks import make_identity

K, T, E, C, N = 384, 1536, 2, 512, 1024
FLOPS = 2 * N * K * (E * C + T)
BYTES = 4 * (N * T + (E + 1) * N * K + 128 * E * C + K * T) + 2 * 128 * (E * C // 16)

F32 = mybir.dt.float32
BF16 = mybir.dt.bfloat16
U32 = mybir.dt.uint32
U16 = mybir.dt.uint16
U8 = mybir.dt.uint8
E4M3 = mybir.dt.float8_e4m3fn_x4
E5M2 = mybir.dt.float8_e5m2_x4
MULT = mybir.AluOpType.mult
ADD = mybir.AluOpType.add

P = 128
PACK = 4
PASSES = N // (P * PACK)
K_TILES = K // P
CHUNK = 512
CHUNKS = T // CHUNK
SHARED = E
RUN = 4


def tile_moe_bds_lin_none_kernel(tc, dyT, w, gate, offs, out):
    nc = tc.nc
    with ExitStack() as ctx:
        keep = ctx.enter_context(tc.tile_pool(name="keep", bufs=1))
        w_ring = ctx.enter_context(tc.tile_pool(name="w_ring", bufs=4))
        raw_ring = ctx.enter_context(tc.tile_pool(name="raw_ring", bufs=3))
        dx_ring = ctx.enter_context(tc.tile_pool(name="dx_ring", bufs=3))
        psum = ctx.enter_context(tc.psum_pool(name="psum", bufs=8))

        dy_rows = dyT.rearrange("(a p t) c -> a p t c", p=P, t=PACK)
        w_rows = w.rearrange("e (a p t) k -> e a p t k", p=P, t=PACK)

        offsets = keep.tile([P, E * C // 16], U16, name="offsets")
        shared_bytes = keep.tile([P, PACK * C], F32, name="shared_bytes", align_bytes=64)
        shared_bytes2 = keep.tile([P, 3072], F32, name="shared_bytes2", align_bytes=64)
        pair_a = keep.tile([P, 4096], F32, name="pair_a")
        pair_b = keep.tile([P, 4352], F32, name="pair_b")
        units = keep.tile([P, 4096], F32, name="units", align_bytes=64)
        gates = [shared_bytes[:, C // 2 : C // 2 + C], shared_bytes2[:, 1536:2048]]
        gate_cols = keep.tile([P, E, PACK], F32, name="gate_cols")
        w_stage = [keep.tile([P, PASSES * K * PACK // 2], F32, name="w_stage", align_bytes=64)[:], shared_bytes2[:, 0:1536]]
        identity = keep.tile([P, P], F32, name="identity")[:]
        planes = {(a, t): keep.tile([P, T], F32, name=f"plane{a}{t}") for a in range(PASSES) for t in range(PACK)}
        windows = [keep.tile([P, T], F32, name=f"window{kt}") for kt in range(K_TILES)]
        w_codes = [keep.tile([P, PASSES * K], U32, name=f"w_codes{m}", align_bytes=64) for m in range(E + 1)]
        w_scales = [keep.tile([P, PASSES * K], U8, name=f"w_scales{m}", align_bytes=64) for m in range(E + 1)]
        g_codes = {(e, a): keep.tile([P, C], U32, name=f"g_codes{e}{a}", align_bytes=64) for e in range(E) for a in range(PASSES)}
        g_scales = {(e, a): keep.tile([P, C], U8, name=f"g_scales{e}{a}", align_bytes=64) for e in range(E) for a in range(PASSES)}
        dy_codes = [keep.tile([P, PASSES * CHUNK], U32, name=f"dy_codes{c}", align_bytes=64) for c in range(CHUNKS)]
        dy_scales = [keep.tile([P, PASSES * CHUNK], U8, name=f"dy_scales{c}", align_bytes=64) for c in range(CHUNKS)]
        dx, ds, ds_banks = {}, {}, {}

        w_raw, dy_raw, g_raw, w_bf, g_bf, dy_bf, dx_banks = {}, {}, {}, {}, {}, {}, {}

        def slots(e):
            return offsets[:, e * C // 16 : (e + 1) * C // 16]

        def load_gate():
            nc.sync.dma_start(gate_cols[:], gate[0, :].rearrange("(e p i) -> p e i", e=E, i=PACK))
            make_identity(nc, identity)

        def spread_gate(e):
            bank = psum.tile([P, CHUNK], F32, name="bank")
            for i in range(PACK):
                nc.tensor.transpose(bank[:, i * P : (i + 1) * P], gate_cols[:, e, i : i + 1].to_broadcast([P, P]), identity)
            nc.vector.tensor_copy(gates[e].rearrange("q (p i) -> q p i", i=PACK), bank[:].rearrange("q (i p) -> q p i", i=PACK))

        def load_plane(a, t):
            nc.sync.dma_start(planes[a, t][:], dy_rows[a, :, t, :])

        def load_w(m, a):
            w_raw[m, a] = w_ring.tile([P, PACK, K], F32, name="w_raw")[:]
            nc.sync.dma_start(w_raw[m, a], w_rows[m, a])

        def load_dy(c, a):
            if c == 0:
                dy_raw[c, a] = pair_a[:].rearrange("p (t h c) -> p t h c", t=PACK, h=2)[:, :, a, :]
            elif (c, a) in ((1, 1), (2, 0)):
                dy_raw[c, a] = pair_b[:, 0:4096].rearrange("p (t h c) -> p t h c", t=PACK, h=2)[:, :, a, :]
            else:
                dy_raw[c, a] = raw_ring.tile([P, PACK, CHUNK], F32, name="raw")[:]
            nc.sync.dma_start(dy_raw[c, a], dy_rows[a, :, :, c * CHUNK : (c + 1) * CHUNK])

        def interleave(dst, src):
            nc.scalar.copy(
                dst.rearrange("p (c i t) -> p c t i", i=RUN, t=PACK),
                src.rearrange("p t (c i) -> p c t i", i=RUN),
            )

        def interleave_gpsimd(dst, src):
            nc.gpsimd.tensor_scalar(dst.rearrange("p (c t) -> p c t", t=PACK), src.rearrange("p t c -> p c t"), 1.0, 0.0, MULT, ADD)

        def gather(e, a, t):
            if t == 0 and (e, a) == (1, 1):
                g_raw[e, a] = shared_bytes[:].rearrange("p (t c) -> p t c", t=PACK)
            elif t == 0:
                g_raw[e, a] = raw_ring.tile([P, PACK, C], F32, name="raw")[:]
            nc.vector.tensor_tensor(g_raw[e, a][:, t, :], planes[a, t][:].indirect(slots(e)), gates[e], MULT)

        def interleave_g(e, a):
            if (e, a) == (0, 1):
                g_bf[e, a] = shared_bytes[:, 2 * C :].bitcast(BF16)
            elif (e, a) == (1, 1):
                g_bf[e, a] = shared_bytes2[:, 2048:3072].bitcast(BF16)
            else:
                g_bf[e, a] = units[:, e * 1024 : (e + 1) * 1024].bitcast(BF16)
            interleave(g_bf[e, a], g_raw[e, a])

        def quantize_g(e, a):
            nc.vector.quantize_mx(g_codes[e, a][:].bitcast(E5M2), g_scales[e, a][:], g_bf[e, a])

        def interleave_w(m, a):
            w_bf[m] = w_stage[m].bitcast(BF16)
            interleave(w_bf[m][:, a * K * PACK : (a + 1) * K * PACK], w_raw[m, a])

        def interleave_w_gpsimd(m, a):
            w_bf[m] = shared_bytes2[:, 1280:2816].bitcast(BF16)
            interleave_gpsimd(w_bf[m][:, a * K * PACK : (a + 1) * K * PACK], w_raw[m, a])

        def quantize_w(m):
            for lo, hi in ((0, 512), (512, PASSES * K)):
                nc.vector.quantize_mx(w_codes[m][:, lo:hi].bitcast(E4M3), w_scales[m][:, lo:hi], w_bf[m][:, PACK * lo : PACK * hi])

        def interleave_dy(c, a):
            dy_bf[c] = (units[:, 1024:3072], units[:, 0:2048], units[:, 2048:4096])[c].bitcast(BF16)
            step = interleave_gpsimd if (c, a) in ((0, 1), (1, 1)) else interleave
            step(dy_bf[c][:, a * CHUNK * PACK : (a + 1) * CHUNK * PACK], dy_raw[c, a])

        def quantize_dy(c):
            nc.vector.quantize_mx(dy_codes[c][:].bitcast(E5M2), dy_scales[c][:], dy_bf[c])

        def product(m, kt, moving):
            bank = psum.tile([P, CHUNK], F32, name="bank")
            for a in range(PASSES):
                cols = slice(a * K + kt * P, a * K + (kt + 1) * P)
                codes, scales = moving(a)
                nc.tensor.matmul_mx(
                    bank[:],
                    lhsT=w_codes[m][:, cols].bitcast(E4M3),
                    lhsT_scale=w_scales[m][:, cols],
                    rhs=codes.bitcast(E5M2),
                    rhs_scale=scales,
                    start=(a == 0),
                    stop=(a == PASSES - 1),
                )
            return bank

        def expert(e, kt):
            dx_banks[e, kt] = product(e, kt, lambda a: (g_codes[e, a][:], g_scales[e, a][:]))

        def evacuate(e, kt):
            if (e, kt) == (1, 1):
                dx[e, kt] = pair_a[:, 256:768]
            elif kt == 2:
                dx[e, kt] = pair_b[:, 256 + e * C : 256 + (e + 1) * C]
            else:
                dx[e, kt] = dx_ring.tile([P, C], F32, name="dx")[:]
            nc.scalar.copy(dx[e, kt], dx_banks[e, kt][:])

        def scatter(e, kt):
            nc.vector.tensor_copy(windows[kt][:].indirect(slots(e)), dx[e, kt])

        def shared(kt, c):
            def moving(a):
                cols = slice(a * CHUNK, (a + 1) * CHUNK)
                return dy_codes[c][:, cols], dy_scales[c][:, cols]

            ds_banks[kt, c] = product(SHARED, kt, moving)

        def evacuate_ds(kt, c):
            place = 2 + 2 * c + kt
            ds[kt, c] = pair_b[:, 256 + place * CHUNK : 256 + (place + 1) * CHUNK]
            nc.scalar.copy(ds[kt, c], ds_banks[kt, c][:])

        def add_gpsimd(kt, c):
            cols = slice(c * CHUNK, (c + 1) * CHUNK)
            if c == 2:
                total = windows[kt][:, cols].rearrange("p (h c) -> p h c", h=2)
            else:
                place = 2 * c + kt
                total = units[:, 1024:3072].rearrange("p (h c) -> p h c", h=2)[:, :, place * 256 : (place + 1) * 256]
            nc.gpsimd.tensor_tensor(
                total, ds[kt, c].rearrange("p (h c) -> p h c", h=2), windows[kt][:, cols].rearrange("p (h c) -> p h c", h=2), ADD
            )
            nc.scalar.dma_start(out[kt * P : (kt + 1) * P, cols].rearrange("p (h c) -> p h c", h=2), total)

        def finish(kt, c):
            shared(kt, c)
            bank = ds_banks[kt, c]
            cols = slice(c * CHUNK, (c + 1) * CHUNK)
            nc.vector.tensor_tensor(windows[kt][:, cols], bank[:], windows[kt][:, cols], ADD)
            nc.sync.dma_start(out[kt * P : (kt + 1) * P, cols], windows[kt][:, cols])

        load_gate()
        nc.sync.dma_start(offsets[:], offs)
        load_plane(0, 0)
        spread_gate(0)
        spread_gate(1)
        load_plane(0, 1)
        load_plane(0, 2)
        load_w(0, 0)
        load_plane(0, 3)
        load_plane(1, 0)
        load_plane(1, 1)
        load_w(0, 1)
        load_plane(1, 2)
        load_plane(1, 3)
        load_w(1, 0)
        load_w(1, 1)
        load_w(2, 0)
        load_w(2, 1)
        nc.gpsimd.memset(windows[0][:], 0.0)
        nc.gpsimd.memset(windows[1][:], 0.0)
        nc.gpsimd.memset(windows[2][:], 0.0)
        gather(0, 0, 0)
        gather(1, 0, 0)
        gather(0, 0, 1)
        gather(1, 0, 1)
        gather(0, 0, 2)
        gather(1, 0, 2)
        gather(0, 0, 3)
        gather(1, 0, 3)
        interleave_w(0, 0)
        interleave_g(0, 0)
        interleave_g(1, 0)
        interleave_w(0, 1)
        gather(0, 1, 0)
        quantize_g(0, 0)
        gather(0, 1, 1)
        quantize_g(1, 0)
        quantize_w(0)
        gather(0, 1, 2)
        gather(0, 1, 3)
        interleave_g(0, 1)
        gather(1, 1, 0)
        gather(1, 1, 1)
        quantize_g(0, 1)
        gather(1, 1, 2)
        gather(1, 1, 3)
        load_dy(2, 1)
        load_dy(0, 0)
        load_dy(0, 1)
        load_dy(1, 0)
        load_dy(1, 1)
        load_dy(2, 0)
        interleave_w(1, 0)
        interleave_w(1, 1)
        quantize_w(1)
        expert(0, 0)
        expert(0, 1)
        expert(0, 2)
        evacuate(0, 0)
        scatter(0, 0)
        interleave_w_gpsimd(2, 0)
        interleave_g(1, 1)
        quantize_g(1, 1)
        interleave_w_gpsimd(2, 1)
        evacuate(0, 1)
        scatter(0, 1)
        expert(1, 0)
        expert(1, 1)
        expert(1, 2)
        interleave_dy(0, 1)
        interleave_dy(2, 1)
        evacuate(1, 0)
        scatter(1, 0)
        quantize_w(2)
        interleave_dy(0, 0)
        interleave_dy(1, 0)
        quantize_dy(0)
        evacuate(1, 1)
        scatter(1, 1)
        interleave_dy(1, 1)
        interleave_dy(2, 0)
        quantize_dy(2)
        quantize_dy(1)
        evacuate(0, 2)
        scatter(0, 2)
        evacuate(1, 2)
        scatter(1, 2)
        shared(0, 0)
        evacuate_ds(0, 0)
        add_gpsimd(0, 0)
        shared(1, 0)
        evacuate_ds(1, 0)
        add_gpsimd(1, 0)
        shared(0, 1)
        evacuate_ds(0, 1)
        add_gpsimd(0, 1)
        shared(1, 1)
        evacuate_ds(1, 1)
        add_gpsimd(1, 1)
        shared(0, 2)
        evacuate_ds(0, 2)
        add_gpsimd(0, 2)
        shared(1, 2)
        evacuate_ds(1, 2)
        add_gpsimd(1, 2)
        finish(2, 0)
        finish(2, 1)
        finish(2, 2)
